import numpy as np
import ml_dtypes


def mxq(x, axis, fmt="e4m3"):
    dtype, down = {"e4m3": (ml_dtypes.float8_e4m3fn, 7), "e5m2": (ml_dtypes.float8_e5m2, 14)}[fmt]
    v = np.moveaxis(np.asarray(x, np.float32).astype(ml_dtypes.bfloat16).astype(np.float64), axis, -1)
    blocks = v.reshape(v.shape[:-1] + (-1, 32))
    amax = np.abs(blocks).max(-1, keepdims=True)
    byte = np.maximum(np.where(amax > 0, np.frexp(amax)[1] - 1 + 127, 0) - down, 1)
    scale = np.exp2(byte - 127.0)
    codes = (blocks / scale).astype(np.float32).astype(dtype).astype(np.float64)
    return np.moveaxis((codes * scale).reshape(v.shape), -1, axis)


WIDE = False


def mx_kscale(k):
    if not WIDE:
        return np.ones(k)
    levels = np.array([10, -10, 5, -5, 0])
    if k % 512:
        return np.exp2(np.random.permutation(np.resize(levels, k // 32))).repeat(32)
    a = np.empty((k // 512, 16))
    for p in range(k // 512):
        a[p, :8] = np.random.permutation(np.resize(levels, 8))
        for g in range(8):
            far = levels[np.abs(levels - a[p, g]) >= 10]
            a[p, g + 8] = far[np.random.randint(len(far))]
    return np.exp2(a.ravel()).repeat(32)


def f64(x):
    return np.asarray(x).astype(np.float64)


def striped8(idx):
    return np.concatenate([v.reshape(-1, 16).T for v in idx]).astype(np.uint16)


def unstriped8(offs):
    return np.stack([offs[16 * g:16 * g + 16].T.reshape(-1) for g in range(8)]).astype(np.int64)


E2M1 = np.array([0.0, 0.5, 1.0, 1.5, 2.0, 3.0, 4.0, 6.0, -0.0, -0.5, -1.0, -1.5, -2.0, -3.0, -4.0, -6.0])


def pack_weight(w, fmt):
    k, n = w.shape
    w = f64(np.asarray(w, np.float32).astype(ml_dtypes.bfloat16)).reshape(k // 32, 32, n)
    amax = np.abs(w).max(1)
    if fmt == "e4m3":
        byte = np.frexp(amax)[1] - 1 + 127 - 7
    else:
        mant, ex = np.frexp(amax / 6.0)
        byte = np.where(mant > 0.5, ex, ex - 1) + 127
    byte = np.clip(np.where(amax > 0, byte, 1), 1, 254)
    scaled = (w * np.exp2(127.0 - byte)[:, None, :]).reshape(k, n).astype(np.float32)
    by_word = np.ascontiguousarray(scaled.reshape(k // 512, 128, 4, n).transpose(0, 1, 3, 2))
    if fmt == "e4m3":
        words = by_word.astype(ml_dtypes.float8_e4m3fn).view(np.uint8)
    else:
        c = by_word.astype(ml_dtypes.float4_e2m1fn).view(np.uint8) & 0xF
        words = (c[..., 0::2] | (c[..., 1::2] << 4)).reshape(k // 512, 128, 2 * n)
    return np.ascontiguousarray(words), np.ascontiguousarray(byte.astype(np.uint8).reshape(k // 512, 16, n))


def unpack_weight(words, scales, fmt):
    g, _, n = scales.shape
    words = np.ascontiguousarray(words).reshape(g, 128, n, -1)
    if fmt == "e4m3":
        vals = words.view(ml_dtypes.float8_e4m3fn).astype(np.float64)
    else:
        nib = np.empty((g, 128, n, 4), np.uint8)
        nib[..., 0::2] = words & 0xF
        nib[..., 1::2] = words >> 4
        vals = E2M1[nib]
    vals = vals * np.repeat(np.exp2(scales.astype(np.float64) - 127.0), 8, axis=1)[..., None]
    return vals.transpose(0, 1, 3, 2).reshape(g * 512, n)


K, M, T, S = 2048, 256, 512, 256


def setup_inputs():
    n = np.random.standard_normal
    s = mx_kscale(K)[:, None]
    p_w = pack_weight(n((K, M)) / np.sqrt(K) / s, "e4m3")
    return {
        "x": (n((K, S)) * s).astype(np.float32),
        "w_words": p_w[0],
        "w_scales": p_w[1],
        "wgo": np.repeat(np.random.uniform(0.5, 2.0, (8, S)), 16, axis=0).astype(np.float32),
        "offs": striped8(np.stack([np.random.permutation(T)[:S] for _ in range(8)])),
    }


def reference(x, w_words, w_scales, wgo, offs):
    x_ = mxq(f64(x), 0, "e4m3")
    w_ = unpack_weight(w_words, w_scales, "e4m3")
    y = w_.T @ x_
    place = unstriped8(offs)[np.arange(M) % 128 // 16]
    out = np.zeros((M, T))
    out[np.arange(M)[:, None], place] = f64(wgo)[np.arange(M) % 128] * (y)
    return out

@@ -1,0 +1,132 @@
+from contextlib import ExitStack
+
+import concourse.mybir as mybir
+
+K, M, S, T = 2048, 256, 256, 512
+FLOPS = 2 * K * M * S
+
+F32 = mybir.dt.float32
+BF16 = mybir.dt.bfloat16
+U32 = mybir.dt.uint32
+I32 = mybir.dt.int32
+U16 = mybir.dt.uint16
+U8 = mybir.dt.uint8
+FP8X4 = mybir.dt.float8_e4m3fn_x4
+MULT = mybir.AluOpType.mult
+
+P = 128
+PACK = 4
+K_PASS = P * PACK
+PASSES = K // K_PASS
+HALF = S // 2
+HALVES = S // HALF
+M_TILES = M // P
+
+
+def tile_list_hscat_none_kernel(tc, x, w_words, w_scales, wgo, offs, out):
+    nc = tc.nc
+    with ExitStack() as ctx:
+        keep = ctx.enter_context(tc.tile_pool(name="keep", bufs=1))
+        psum = ctx.enter_context(tc.psum_pool(name="psum", bufs=1))
+
+        def load_x(a, c0, width):
+            raw = keep.tile([P, PACK, width], F32, name=f"raw_{a}_{c0}", align_bytes=64)
+            rows = x[a * K_PASS : (a + 1) * K_PASS, c0 : c0 + width]
+            nc.sync.dma_start(out=raw[:], in_=rows.rearrange("(p j) w -> p j w", j=PACK))
+            grouped = keep.tile([P, width, PACK], BF16, name=f"grouped_{a}_{c0}", align_bytes=64)
+            return raw, grouped
+
+        def interleave(copy, chunk, c0, c1):
+            raw, grouped = chunk
+            copy(
+                out=grouped[:, c0:c1, :].rearrange("p (c i) t -> p c t i", i=4),
+                in_=raw[:, :, c0:c1].rearrange("p t (c i) -> p c t i", i=4),
+            )
+
+        def quantize(a, c0, width, chunk):
+            codes = keep.tile([P, width], U32, name=f"codes_{a}_{c0}", align_bytes=64)
+            scales = keep.tile([P, width], U8, name=f"scales_{a}_{c0}", align_bytes=64)
+            nc.vector.quantize_mx(
+                out=codes[:].bitcast(FP8X4),
+                scales=scales[:],
+                in_=chunk[1][:].rearrange("p w t -> p (w t)"),
+            )
+            return codes, scales
+
+        packed = keep.tile([P, M], U8, name="packed", align_bytes=64)
+        nc.vector.memset(packed[:].bitcast(I32), 0)
+        windows = [keep.tile([P, T], F32, name=f"window_{m}", align_bytes=64) for m in range(M_TILES)]
+        for m in range(M_TILES):
+            nc.gpsimd.memset(windows[m][:], 0.0)
+
+        x0 = load_x(0, 0, S)
+        offsets = keep.tile([P, S // 16], U16, name="offsets")
+        nc.sync.dma_start(offsets[:], offs)
+        for q in range(4):
+            nc.scalar.dma_start(
+                out=packed[32 * q : 32 * q + 16, :].bitcast(I32),
+                in_=w_scales[:, 4 * q : 4 * q + 4, :].bitcast(I32),
+            )
+        x1 = load_x(1, 0, S)
+        words = keep.tile([P, PASSES, M], U32, name="words", align_bytes=64)
+        nc.sync.dma_start(
+            out=words[:].bitcast(I32),
+            in_=w_words.rearrange("a p n t -> p a (n t)").bitcast(I32),
+        )
+        x2 = load_x(2, 0, S)
+        x3 = [None, None]
+        x3[0] = load_x(3, 0, HALF)
+        weights = keep.tile([P, S], F32, name="weights", align_bytes=64)
+        nc.sync.dma_start(out=weights[:], in_=wgo)
+        x3[1] = load_x(3, HALF, HALF)
+
+        acc = [[psum.tile([P, HALF], F32, name=f"acc_{m}_{h}") for h in range(HALVES)] for m in range(M_TILES)]
+
+        def multiply(a, m, h, codes, scales, c0):
+            nc.tensor.matmul_mx(
+                out=acc[m][h][:],
+                lhsT=words[:, a, m * P : (m + 1) * P].bitcast(FP8X4),
+                lhsT_scale=packed[4 * a :, m * P : (m + 1) * P],
+                rhs=codes[:, c0 : c0 + HALF].bitcast(FP8X4),
+                rhs_scale=scales[:, c0 : c0 + HALF],
+                start=(a == 0),
+                stop=(a == PASSES - 1),
+            )
+
+        for a, chunk in enumerate((x0, x1, x2)):
+            interleave(nc.vector.tensor_copy, chunk, 0, 128)
+            interleave(nc.scalar.copy, chunk, 128, S)
+            codes, scales = quantize(a, 0, S, chunk)
+            for h in range(HALVES):
+                for m in range(M_TILES):
+                    multiply(a, m, h, codes, scales, h * HALF)
+
+        results = [[keep.tile([P, HALF], F32, name=f"y_{m}_{h}", align_bytes=64) for h in range(HALVES)] for m in range(M_TILES)]
+
+        def place(m, h):
+            nc.vector.tensor_tensor(
+                windows[m][:].indirect(offsets[:, 8 * h : 8 * h + 8]),
+                results[m][h][:],
+                weights[:, h * HALF : (h + 1) * HALF],
+                MULT,
+            )
+
+        interleave(nc.vector.tensor_copy, x3[0], 0, 56)
+        interleave(nc.scalar.copy, x3[0], 56, HALF)
+        codes, scales = quantize(3, 0, HALF, x3[0])
+        for m in range(M_TILES):
+            multiply(3, m, 0, codes, scales, 0)
+        for m in range(M_TILES):
+            nc.scalar.copy(out=results[m][0][:], in_=acc[m][0][:])
+        place(0, 0)
+
+        interleave(nc.scalar.copy, x3[1], 0, HALF)
+        codes, scales = quantize(3, HALF, HALF, x3[1])
+        place(1, 0)
+        for m in range(M_TILES):
+            multiply(3, m, 1, codes, scales, 0)
+        for m in range(M_TILES):
+            nc.scalar.copy(out=results[m][1][:], in_=acc[m][1][:])
+        for m in range(M_TILES):
+            place(m, 1)
+            nc.sync.dma_start(out=out[m * P : (m + 1) * P, :], in_=windows[m][:])

@@ -59,49 +59,47 @@ def tile_list_hscat_none_kernel(tc, x, w_words, w_scales, wgo, offs, out):
         for m in range(M_TILES):
             nc.gpsimd.memset(windows[m][:], 0.0)
 
-        x0 = load_x(0, 0, S)
         offsets = keep.tile([P, S // 16], U16, name="offsets")
-        nc.sync.dma_start(offsets[:], offs)
+        weights = keep.tile([P, S], F32, name="weights", align_bytes=64)
+        words = [keep.tile([P, PASSES, P], U32, name=f"words_{m}", align_bytes=64) for m in range(M_TILES)]
+
+        def load_w(m):
+            nc.sync.dma_start(
+                out=words[m][:].bitcast(I32),
+                in_=w_words[:, :, m * P : (m + 1) * P, :].rearrange("a p n t -> p a (n t)").bitcast(I32),
+            )
+
+        x3 = [None, None]
         for q in range(4):
             nc.scalar.dma_start(
                 out=packed[32 * q : 32 * q + 16, :].bitcast(I32),
                 in_=w_scales[:, 4 * q : 4 * q + 4, :].bitcast(I32),
             )
+        x0 = load_x(0, 0, S)
+        nc.sync.dma_start(offsets[:], offs)
+        load_w(0)
         x1 = load_x(1, 0, S)
-        words = keep.tile([P, PASSES, M], U32, name="words", align_bytes=64)
-        nc.sync.dma_start(
-            out=words[:].bitcast(I32),
-            in_=w_words.rearrange("a p n t -> p a (n t)").bitcast(I32),
-        )
         x2 = load_x(2, 0, S)
-        x3 = [None, None]
         x3[0] = load_x(3, 0, HALF)
-        weights = keep.tile([P, S], F32, name="weights", align_bytes=64)
         nc.sync.dma_start(out=weights[:], in_=wgo)
         x3[1] = load_x(3, HALF, HALF)
+        load_w(1)
 
         acc = [[psum.tile([P, HALF], F32, name=f"acc_{m}_{h}") for h in range(HALVES)] for m in range(M_TILES)]
+        results = [[keep.tile([P, HALF], F32, name=f"y_{m}_{h}", align_bytes=64) for h in range(HALVES)] for m in range(M_TILES)]
+        quantized = {}
 
-        def multiply(a, m, h, codes, scales, c0):
+        def multiply(a, m, h):
+            codes, scales, c0 = quantized[a, h]
             nc.tensor.matmul_mx(
                 out=acc[m][h][:],
-                lhsT=words[:, a, m * P : (m + 1) * P].bitcast(FP8X4),
+                lhsT=words[m][:, a, :].bitcast(FP8X4),
                 lhsT_scale=packed[4 * a :, m * P : (m + 1) * P],
                 rhs=codes[:, c0 : c0 + HALF].bitcast(FP8X4),
                 rhs_scale=scales[:, c0 : c0 + HALF],
                 start=(a == 0),
                 stop=(a == PASSES - 1),
             )
-
-        for a, chunk in enumerate((x0, x1, x2)):
-            interleave(nc.vector.tensor_copy, chunk, 0, 128)
-            interleave(nc.scalar.copy, chunk, 128, S)
-            codes, scales = quantize(a, 0, S, chunk)
-            for h in range(HALVES):
-                for m in range(M_TILES):
-                    multiply(a, m, h, codes, scales, h * HALF)
-
-        results = [[keep.tile([P, HALF], F32, name=f"y_{m}_{h}", align_bytes=64) for h in range(HALVES)] for m in range(M_TILES)]
 
         def place(m, h):
             nc.vector.tensor_tensor(
@@ -111,22 +109,35 @@ def tile_list_hscat_none_kernel(tc, x, w_words, w_scales, wgo, offs, out):
                 MULT,
             )
 
+        def store(m):
+            nc.sync.dma_start(out=out[m * P : (m + 1) * P, :], in_=windows[m][:])
+
+        for a, chunk in enumerate((x0, x1, x2)):
+            interleave(nc.vector.tensor_copy, chunk, 0, 128)
+            interleave(nc.scalar.copy, chunk, 128, S)
+            codes, scales = quantize(a, 0, S, chunk)
+            for h in range(HALVES):
+                quantized[a, h] = (codes, scales, h * HALF)
+                multiply(a, 0, h)
+
         interleave(nc.vector.tensor_copy, x3[0], 0, 56)
         interleave(nc.scalar.copy, x3[0], 56, HALF)
-        codes, scales = quantize(3, 0, HALF, x3[0])
-        for m in range(M_TILES):
-            multiply(3, m, 0, codes, scales, 0)
-        for m in range(M_TILES):
-            nc.scalar.copy(out=results[m][0][:], in_=acc[m][0][:])
+        quantized[3, 0] = (*quantize(3, 0 * HALF, HALF, x3[0]), 0)
+        multiply(3, 0, 0)
+        nc.scalar.copy(out=results[0][0][:], in_=acc[0][0][:])
         place(0, 0)
-
         interleave(nc.scalar.copy, x3[1], 0, HALF)
-        codes, scales = quantize(3, HALF, HALF, x3[1])
+        quantized[3, 1] = (*quantize(3, 1 * HALF, HALF, x3[1]), 0)
+        for a in range(PASSES):
+            multiply(a, 1, 0)
+        multiply(3, 0, 1)
+        nc.scalar.copy(out=results[1][0][:], in_=acc[1][0][:])
         place(1, 0)
-        for m in range(M_TILES):
-            multiply(3, m, 1, codes, scales, 0)
-        for m in range(M_TILES):
-            nc.scalar.copy(out=results[m][1][:], in_=acc[m][1][:])
-        for m in range(M_TILES):
-            place(m, 1)
-            nc.sync.dma_start(out=out[m * P : (m + 1) * P, :], in_=windows[m][:])
+        nc.scalar.copy(out=results[0][1][:], in_=acc[0][1][:])
+        place(0, 1)
+        store(0)
+        for a in range(PASSES):
+            multiply(a, 1, 1)
+        nc.scalar.copy(out=results[1][1][:], in_=acc[1][1][:])
+        place(1, 1)
+        store(1)

@@ -54,7 +54,7 @@ def tile_list_hscat_none_kernel(tc, x, w_words, w_scales, wgo, offs, out):
             return codes, scales
 
         packed = keep.tile([P, M], U8, name="packed", align_bytes=64)
-        nc.vector.memset(packed[:].bitcast(I32), 0)
+        nc.gpsimd.memset(packed[:].bitcast(I32), 0)
         windows = [keep.tile([P, T], F32, name=f"window_{m}", align_bytes=64) for m in range(M_TILES)]
         for m in range(M_TILES):
             nc.gpsimd.memset(windows[m][:], 0.0)
@@ -69,20 +69,25 @@ def tile_list_hscat_none_kernel(tc, x, w_words, w_scales, wgo, offs, out):
                 in_=w_words[:, :, m * P : (m + 1) * P, :].rearrange("a p n t -> p a (n t)").bitcast(I32),
             )
 
-        x3 = [None, None]
-        for q in range(4):
-            nc.scalar.dma_start(
+        def load_scales(q):
+            nc.sync.dma_start(
                 out=packed[32 * q : 32 * q + 16, :].bitcast(I32),
                 in_=w_scales[:, 4 * q : 4 * q + 4, :].bitcast(I32),
             )
-        x0 = load_x(0, 0, S)
+
+        x_in = {}
         nc.sync.dma_start(offsets[:], offs)
+        x_in[0, 0] = load_x(0, 0, S)
+        load_scales(0)
+        load_scales(1)
+        load_scales(2)
+        load_scales(3)
+        x_in[1, 0] = load_x(1, 0, S)
+        x_in[2, 0] = load_x(2, 0, S)
         load_w(0)
-        x1 = load_x(1, 0, S)
-        x2 = load_x(2, 0, S)
-        x3[0] = load_x(3, 0, HALF)
+        x_in[3, 0] = load_x(3, 0 * HALF, HALF)
         nc.sync.dma_start(out=weights[:], in_=wgo)
-        x3[1] = load_x(3, HALF, HALF)
+        x_in[3, 1] = load_x(3, 1 * HALF, HALF)
         load_w(1)
 
         acc = [[psum.tile([P, HALF], F32, name=f"acc_{m}_{h}") for h in range(HALVES)] for m in range(M_TILES)]
@@ -112,32 +117,49 @@ def tile_list_hscat_none_kernel(tc, x, w_words, w_scales, wgo, offs, out):
         def store(m):
             nc.sync.dma_start(out=out[m * P : (m + 1) * P, :], in_=windows[m][:])
 
-        for a, chunk in enumerate((x0, x1, x2)):
-            interleave(nc.vector.tensor_copy, chunk, 0, 128)
-            interleave(nc.scalar.copy, chunk, 128, S)
-            codes, scales = quantize(a, 0, S, chunk)
-            for h in range(HALVES):
-                quantized[a, h] = (codes, scales, h * HALF)
-                multiply(a, 0, h)
+        def cast(a, h, width, vector_cols):
+            if vector_cols > 0:
+                interleave(nc.vector.tensor_copy, x_in[a, h], 0, vector_cols)
+            if vector_cols < width:
+                interleave(nc.scalar.copy, x_in[a, h], vector_cols, width)
 
-        interleave(nc.vector.tensor_copy, x3[0], 0, 56)
-        interleave(nc.scalar.copy, x3[0], 56, HALF)
-        quantized[3, 0] = (*quantize(3, 0 * HALF, HALF, x3[0]), 0)
+        def fetch(m, h):
+            nc.scalar.copy(out=results[m][h][:], in_=acc[m][h][:])
+
+        def quant(a, h, width):
+            codes, scales = quantize(a, h * HALF, width, x_in[a, h])
+            for i in range(width // HALF):
+                quantized[a, h + i] = (codes, scales, i * HALF)
+
+        cast(0, 0, S, 176)
+        quant(0, 0, S)
+        multiply(0, 0, 0)
+        multiply(0, 0, 1)
+        cast(1, 0, S, 176)
+        quant(1, 0, S)
+        multiply(1, 0, 0)
+        multiply(1, 0, 1)
+        cast(2, 0, S, 176)
+        quant(2, 0, S)
+        multiply(2, 0, 0)
+        multiply(2, 0, 1)
+        cast(3, 0, HALF, 44)
+        quant(3, 0, HALF)
         multiply(3, 0, 0)
-        nc.scalar.copy(out=results[0][0][:], in_=acc[0][0][:])
+        fetch(0, 0)
         place(0, 0)
-        interleave(nc.scalar.copy, x3[1], 0, HALF)
-        quantized[3, 1] = (*quantize(3, 1 * HALF, HALF, x3[1]), 0)
+        cast(3, 1, HALF, 0)
+        quant(3, 1, HALF)
         for a in range(PASSES):
             multiply(a, 1, 0)
+        fetch(1, 0)
         multiply(3, 0, 1)
-        nc.scalar.copy(out=results[1][0][:], in_=acc[1][0][:])
         place(1, 0)
-        nc.scalar.copy(out=results[0][1][:], in_=acc[0][1][:])
+        fetch(0, 1)
         place(0, 1)
         store(0)
         for a in range(PASSES):
             multiply(a, 1, 1)
-        nc.scalar.copy(out=results[1][1][:], in_=acc[1][1][:])
+        fetch(1, 1)
         place(1, 1)
         store(1)

from contextlib import ExitStack

import concourse.mybir as mybir

K, M, S, T = 2048, 256, 256, 512
FLOPS = 2 * K * M * S

F32 = mybir.dt.float32
BF16 = mybir.dt.bfloat16
U32 = mybir.dt.uint32
I32 = mybir.dt.int32
U16 = mybir.dt.uint16
U8 = mybir.dt.uint8
FP8X4 = mybir.dt.float8_e4m3fn_x4
MULT = mybir.AluOpType.mult

P = 128
PACK = 4
K_PASS = P * PACK
PASSES = K // K_PASS
HALF = S // 2
HALVES = S // HALF
M_TILES = M // P


def tile_list_hscat_none_kernel(tc, x, w_words, w_scales, wgo, offs, out):
    nc = tc.nc
    with ExitStack() as ctx:
        keep = ctx.enter_context(tc.tile_pool(name="keep", bufs=1))
        psum = ctx.enter_context(tc.psum_pool(name="psum", bufs=1))

        def load_x(a, c0, width):
            raw = keep.tile([P, PACK, width], F32, name=f"raw_{a}_{c0}", align_bytes=64)
            rows = x[a * K_PASS : (a + 1) * K_PASS, c0 : c0 + width]
            nc.sync.dma_start(out=raw[:], in_=rows.rearrange("(p j) w -> p j w", j=PACK))
            grouped = keep.tile([P, width, PACK], BF16, name=f"grouped_{a}_{c0}", align_bytes=64)
            return raw, grouped

        def interleave(copy, chunk, c0, c1):
            raw, grouped = chunk
            copy(
                out=grouped[:, c0:c1, :].rearrange("p (c i) t -> p c t i", i=4),
                in_=raw[:, :, c0:c1].rearrange("p t (c i) -> p c t i", i=4),
            )

        def quantize(a, c0, width, chunk):
            codes = keep.tile([P, width], U32, name=f"codes_{a}_{c0}", align_bytes=64)
            scales = keep.tile([P, width], U8, name=f"scales_{a}_{c0}", align_bytes=64)
            nc.vector.quantize_mx(
                out=codes[:].bitcast(FP8X4),
                scales=scales[:],
                in_=chunk[1][:].rearrange("p w t -> p (w t)"),
            )
            return codes, scales

        packed = keep.tile([P, M], U8, name="packed", align_bytes=64)
        nc.gpsimd.memset(packed[:].bitcast(I32), 0)
        windows = [keep.tile([P, T], F32, name=f"window_{m}", align_bytes=64) for m in range(M_TILES)]
        for m in range(M_TILES):
            nc.gpsimd.memset(windows[m][:], 0.0)

        offsets = keep.tile([P, S // 16], U16, name="offsets")
        weights = keep.tile([P, S], F32, name="weights", align_bytes=64)
        words = [keep.tile([P, PASSES, P], U32, name=f"words_{m}", align_bytes=64) for m in range(M_TILES)]

        def load_w(m):
            nc.sync.dma_start(
                out=words[m][:].bitcast(I32),
                in_=w_words[:, :, m * P : (m + 1) * P, :].rearrange("a p n t -> p a (n t)").bitcast(I32),
            )

        def load_scales(q):
            nc.sync.dma_start(
                out=packed[32 * q : 32 * q + 16, :].bitcast(I32),
                in_=w_scales[:, 4 * q : 4 * q + 4, :].bitcast(I32),
            )

        x_in = {}
        nc.sync.dma_start(offsets[:], offs)
        x_in[0, 0] = load_x(0, 0, S)
        load_scales(0)
        load_scales(1)
        load_scales(2)
        load_scales(3)
        x_in[1, 0] = load_x(1, 0, S)
        x_in[2, 0] = load_x(2, 0, S)
        load_w(0)
        x_in[3, 0] = load_x(3, 0 * HALF, HALF)
        nc.sync.dma_start(out=weights[:], in_=wgo)
        x_in[3, 1] = load_x(3, 1 * HALF, HALF)
        load_w(1)

        acc = [[psum.tile([P, HALF], F32, name=f"acc_{m}_{h}") for h in range(HALVES)] for m in range(M_TILES)]
        results = [[keep.tile([P, HALF], F32, name=f"y_{m}_{h}", align_bytes=64) for h in range(HALVES)] for m in range(M_TILES)]
        quantized = {}

        def multiply(a, m, h):
            codes, scales, c0 = quantized[a, h]
            nc.tensor.matmul_mx(
                out=acc[m][h][:],
                lhsT=words[m][:, a, :].bitcast(FP8X4),
                lhsT_scale=packed[4 * a :, m * P : (m + 1) * P],
                rhs=codes[:, c0 : c0 + HALF].bitcast(FP8X4),
                rhs_scale=scales[:, c0 : c0 + HALF],
                start=(a == 0),
                stop=(a == PASSES - 1),
            )

        def place(m, h):
            nc.vector.tensor_tensor(
                windows[m][:].indirect(offsets[:, 8 * h : 8 * h + 8]),
                results[m][h][:],
                weights[:, h * HALF : (h + 1) * HALF],
                MULT,
            )

        def store(m):
            nc.sync.dma_start(out=out[m * P : (m + 1) * P, :], in_=windows[m][:])

        def cast(a, h, width, vector_cols):
            if vector_cols > 0:
                interleave(nc.vector.tensor_copy, x_in[a, h], 0, vector_cols)
            if vector_cols < width:
                interleave(nc.scalar.copy, x_in[a, h], vector_cols, width)

        def fetch(m, h):
            nc.scalar.copy(out=results[m][h][:], in_=acc[m][h][:])

        def quant(a, h, width):
            codes, scales = quantize(a, h * HALF, width, x_in[a, h])
            for i in range(width // HALF):
                quantized[a, h + i] = (codes, scales, i * HALF)

        cast(0, 0, S, 176)
        quant(0, 0, S)
        multiply(0, 0, 0)
        multiply(0, 0, 1)
        cast(1, 0, S, 176)
        quant(1, 0, S)
        multiply(1, 0, 0)
        multiply(1, 0, 1)
        cast(2, 0, S, 176)
        quant(2, 0, S)
        multiply(2, 0, 0)
        multiply(2, 0, 1)
        cast(3, 0, HALF, 44)
        quant(3, 0, HALF)
        multiply(3, 0, 0)
        fetch(0, 0)
        place(0, 0)
        cast(3, 1, HALF, 0)
        quant(3, 1, HALF)
        for a in range(PASSES):
            multiply(a, 1, 0)
        fetch(1, 0)
        multiply(3, 0, 1)
        place(1, 0)
        fetch(0, 1)
        place(0, 1)
        store(0)
        for a in range(PASSES):
            multiply(a, 1, 1)
        fetch(1, 1)
        place(1, 1)
        store(1)
